import numpy as np
import ml_dtypes


def mxq(x, axis, fmt="e4m3"):
    dtype, down = {"e4m3": (ml_dtypes.float8_e4m3fn, 7), "e5m2": (ml_dtypes.float8_e5m2, 14)}[fmt]
    v = np.moveaxis(np.asarray(x, np.float32).astype(ml_dtypes.bfloat16).astype(np.float64), axis, -1)
    blocks = v.reshape(v.shape[:-1] + (-1, 32))
    amax = np.abs(blocks).max(-1, keepdims=True)
    byte = np.maximum(np.where(amax > 0, np.frexp(amax)[1] - 1 + 127, 0) - down, 1)
    scale = np.exp2(byte - 127.0)
    codes = (blocks / scale).astype(np.float32).astype(dtype).astype(np.float64)
    return np.moveaxis((codes * scale).reshape(v.shape), -1, axis)


WIDE = False


def mx_kscale(k):
    if not WIDE:
        return np.ones(k)
    levels = np.array([10, -10, 5, -5, 0])
    if k % 512:
        return np.exp2(np.random.permutation(np.resize(levels, k // 32))).repeat(32)
    a = np.empty((k // 512, 16))
    for p in range(k // 512):
        a[p, :8] = np.random.permutation(np.resize(levels, 8))
        for g in range(8):
            far = levels[np.abs(levels - a[p, g]) >= 10]
            a[p, g + 8] = far[np.random.randint(len(far))]
    return np.exp2(a.ravel()).repeat(32)


def f64(x):
    return np.asarray(x).astype(np.float64)


def striped(idx):
    return np.tile(idx.reshape(-1, 16).T, (8, 1)).astype(np.uint16)


def unstriped(offs):
    return offs[:16].T.reshape(-1).astype(np.int64)


def pack_weight(w):
    k, n = w.shape
    w = f64(np.asarray(w, np.float32).astype(ml_dtypes.bfloat16)).reshape(k // 32, 32, n)
    amax = np.abs(w).max(1)
    byte = np.clip(np.where(amax > 0, np.frexp(amax)[1] - 1 + 127 - 7, 1), 1, 254)
    scaled = (w * np.exp2(127.0 - byte)[:, None, :]).reshape(k, n).astype(np.float32)
    words = np.ascontiguousarray(scaled.reshape(k // 512, 128, 4, n).transpose(0, 1, 3, 2)).astype(ml_dtypes.float8_e4m3fn).view(np.uint8)
    return words, np.ascontiguousarray(byte.astype(np.uint8).reshape(k // 512, 16, n))


def unpack_weight(words, scales):
    g, p, n, _ = words.shape
    vals = np.ascontiguousarray(words).view(ml_dtypes.float8_e4m3fn).astype(np.float64) * np.repeat(np.exp2(scales.astype(np.float64) - 127.0), 8, axis=1)[..., None]
    return vals.transpose(0, 1, 3, 2).reshape(g * 512, n)


K, T, D, H, N = 1024, 512, 3, 512, 256
P = 2 ** 7


def setup_inputs():
    n = np.random.standard_normal
    s = mx_kscale(K)[:, None]
    u = mx_kscale(H)
    packed_xT = pack_weight(n((K, T)) * s)
    packed_w2 = pack_weight(n((H, N)) / np.sqrt(H) / u[:, None])
    return {
        "x_words": packed_xT[0],
        "x_scales": packed_xT[1],
        "w1": (n((K, H)) / np.sqrt(K) / s * u).astype(np.float32),
        "w2_words": packed_w2[0],
        "w2_scales": packed_w2[1],
        "gate": (np.tile(np.random.uniform(0.2, 1.0, (D, 1, T)) / np.sqrt(D), (1, P, 1))).astype(np.float32),
        "pos1": striped(np.random.permutation(T)),
        "pos2": striped(np.random.permutation(T)),
        "pos3": striped(np.random.permutation(T)),
    }


def reference(x_words, x_scales, w1, w2_words, w2_scales, gate, pos1, pos2, pos3):
    xq = unpack_weight(x_words, x_scales)
    h = mxq(f64(w1), 0, "e4m3").T @ xq
    z = h - (h[:, unstriped(pos1)] * f64(gate)[0, :1] + h[:, unstriped(pos2)] * f64(gate)[1, :1] + h[:, unstriped(pos3)] * f64(gate)[2, :1])
    return unpack_weight(w2_words, w2_scales).T @ mxq(z, 0, "e4m3")

@@ -1,0 +1,236 @@
+from contextlib import ExitStack
+
+import concourse.mybir as mybir
+from concourse.masks import make_identity
+
+K, T, D, H, N = 1024, 512, 3, 512, 256
+FLOPS = 2 * K * H * T + 2 * H * N * T
+
+F32 = mybir.dt.float32
+BF16 = mybir.dt.bfloat16
+I32 = mybir.dt.int32
+U32 = mybir.dt.uint32
+U16 = mybir.dt.uint16
+U8 = mybir.dt.uint8
+FP8X4 = mybir.dt.float8_e4m3fn_x4
+COPY = mybir.ActivationFunctionType.Copy
+MULT = mybir.AluOpType.mult
+
+P = 128
+PACK = 4
+PASSES = K // (P * PACK)
+BLOCKS = H // P
+VBLOCKS = T // P
+SPARE = 16
+
+
+def tile_picked_wlapl_none_l_kernel(
+    tc, x_words, x_scales, w1, w2_words, w2_scales, gate, pos1, pos2, pos3, out
+):
+    nc = tc.nc
+    with ExitStack() as ctx:
+        keep = ctx.enter_context(tc.tile_pool(name="keep", bufs=1))
+        sums = ctx.enter_context(tc.psum_pool(name="sums", bufs=1))
+        work = ctx.enter_context(tc.psum_pool(name="work", bufs=4))
+
+        x_plane = keep.tile([P, PASSES, T], U8, name="x_plane", align_bytes=64)
+        w2_plane = keep.tile([P, N], U8, name="w2_plane", align_bytes=64)
+        nc.gpsimd.memset(x_plane[:].rearrange("p g c -> p (g c)").bitcast(U32), 0)
+        nc.gpsimd.memset(w2_plane[:].bitcast(U32), 0)
+        ident = keep.tile([P, P], F32, name="ident")
+        make_identity(nc, ident[:])
+        h = [keep.tile([P, T + SPARE], F32, name="h%d" % j) for j in range(BLOCKS)]
+        for j in range(BLOCKS):
+            nc.gpsimd.memset(h[j][:, T:], 0.0)
+
+        w1_raw = {}
+
+        def load_w1(j0, j1, g):
+            raw = keep.tile([P, PACK, (j1 - j0) * P], F32, name="w1_raw%d_%d" % (j0, g))
+            rows = w1[g * P * PACK : (g + 1) * P * PACK, j0 * P : j1 * P]
+            nc.sync.dma_start(out=raw[:], in_=rows.rearrange("(p t) c -> p t c", t=PACK))
+            for j in range(j0, j1):
+                w1_raw[j, g] = raw[:, :, (j - j0) * P : (j - j0 + 1) * P]
+
+        def load_list(d, pos):
+            offsets = keep.tile([P, T // 16], U16, name="offsets%d" % d)
+            nc.sync.dma_start(offsets[:], pos)
+            return offsets
+
+        for g in range(PASSES):
+            load_w1(0, 2, g)
+        for q in range(4):
+            (nc.scalar if q < 2 else nc.sync).dma_start(
+                out=x_plane[32 * q : 32 * q + 4].bitcast(I32),
+                in_=x_scales[:, 4 * q : 4 * q + 4, :].rearrange("g r c -> r g c").bitcast(I32),
+            )
+        x_codes = []
+        for g in range(PASSES):
+            codes = keep.tile([P, T], U32, name="x_codes%d" % g, align_bytes=64)
+            nc.sync.dma_start(out=codes[:].bitcast(I32), in_=x_words[g].rearrange("p c r -> p (c r)").bitcast(I32))
+            x_codes.append(codes)
+        lists = [load_list(0, pos1)]
+        gate_first = keep.tile([P, T], F32, name="gate_first")
+        gate_rest = keep.tile([P, D - 1, T], F32, name="gate_rest")
+        gates = [gate_first[:]] + [gate_rest[:, d, :] for d in range(D - 1)]
+        nc.sync.dma_start(out=gate_first[:], in_=gate[0])
+        lists.append(load_list(1, pos2))
+        lists.append(load_list(2, pos3))
+        nc.sync.dma_start(out=gate_rest[:], in_=gate[1:].rearrange("d p v -> p d v"))
+        for g in range(PASSES):
+            load_w1(2, BLOCKS, g)
+        w2_codes = keep.tile([P, N], U32, name="w2_codes", align_bytes=64)
+        nc.sync.dma_start(out=w2_codes[:].bitcast(I32), in_=w2_words[0].rearrange("p c r -> p (c r)").bitcast(I32))
+        for q in range(4):
+            nc.sync.dma_start(
+                out=w2_plane[32 * q : 32 * q + 4].bitcast(I32),
+                in_=w2_scales[0, 4 * q : 4 * q + 4, :].bitcast(I32),
+            )
+
+        def weave(engine_copy, dst, raw):
+            engine_copy(
+                out=dst.rearrange("p (c i t) -> p c t i", i=4, t=PACK),
+                in_=raw.rearrange("p t (c i) -> p c t i", i=4),
+            )
+
+        w1_codes = [keep.tile([P, PASSES, P], U32, name="w1_codes%d" % j, tag="chain%d" % j, align_bytes=64) for j in range(BLOCKS)]
+        w1_plane = [keep.tile([P, PASSES, P], U8, name="w1_plane%d" % j, align_bytes=64) for j in range(BLOCKS)]
+
+        def quantize_w1_first():
+            for g in range(PASSES):
+                woven = [keep.tile([P, P * PACK], BF16, name="w1_first%d_%d" % (j, g), align_bytes=64) for j in range(2)]
+                for j in range(2):
+                    weave(nc.vector.tensor_copy, woven[j][:], w1_raw[j, g])
+                for j in range(2):
+                    nc.vector.quantize_mx(
+                        out=w1_codes[j][:, g, :].bitcast(FP8X4), scales=w1_plane[j][:, g, :], in_=woven[j][:]
+                    )
+
+        def quantize_w1(j, engine_copy, tag):
+            woven = keep.tile([P, PASSES, P * PACK], BF16, name="w1_woven%d" % j, tag=tag, align_bytes=64)
+            for g in range(PASSES):
+                weave(engine_copy, woven[:, g, :], w1_raw[j, g])
+            nc.vector.quantize_mx(
+                out=w1_codes[j][:].rearrange("p g c -> p (g c)").bitcast(FP8X4),
+                scales=w1_plane[j][:].rearrange("p g c -> p (g c)"),
+                in_=woven[:].rearrange("p g c -> p (g c)"),
+            )
+
+        minus_h = [keep.tile([P, T], F32, name="minus_h%d" % j) for j in range(BLOCKS)]
+
+        def project(j):
+            acc = work.tile([P, T], F32, name="h_acc%d" % j, tag="work")
+            for g in range(PASSES):
+                nc.tensor.matmul_mx(
+                    out=acc[:],
+                    lhsT=w1_codes[j][:, g, :].bitcast(FP8X4),
+                    lhsT_scale=w1_plane[j][:, g, :],
+                    rhs=x_codes[g][:].bitcast(FP8X4),
+                    rhs_scale=x_plane[:, g, :],
+                    start=(g == 0),
+                    stop=(g == PASSES - 1),
+                )
+            nc.scalar.copy(out=h[j][:, :T], in_=acc[:])
+            return acc
+
+        def negate(j, acc):
+            nc.scalar.activation(out=minus_h[j][:], in_=acc[:], func=COPY, scale=-1.0)
+
+        turned = [sums.tile([P, H], F32, name="turned%d" % b) for b in range(VBLOCKS)]
+        z_rows = [keep.tile([P, 2, P, 2], BF16, name="z_rows%d" % b, tag="rows%d" % b, align_bytes=64) for b in range(VBLOCKS)]
+
+        def add_turned(j, b, term, first, last):
+            nc.tensor.matmul(
+                out=turned[b][:, j * P : (j + 1) * P], lhsT=term, rhs=ident[:], start=first, stop=last, is_transpose=True
+            )
+
+        def gather(j, d, b0, b1, tag=None):
+            v0, v1 = b0 * P, b1 * P
+            term = keep.tile([P, v1 - v0], F32, name="term%d_%d_%d" % (j, d, b0), tag=tag or "term%d_%d_%d" % (j, d, b0), align_bytes=64)
+            window = h[j][:].indirect(lists[d][:, v0 // 16 : v1 // 16])
+            nc.vector.tensor_tensor(term[:], window, gates[d][:, v0:v1], MULT)
+            for b in range(b0, b1):
+                if d == 0:
+                    add_turned(j, b, minus_h[j][:, b * P : (b + 1) * P], True, False)
+                add_turned(j, b, term[:, (b - b0) * P : (b - b0 + 1) * P], False, d == D - 1)
+
+        def round_z(b, j0, j1):
+            nc.scalar.activation(
+                out=z_rows[b][:, :, 32 * j0 : 32 * j1, :],
+                in_=turned[b][:, j0 * P : j1 * P].rearrange("v (p u e) -> v u p e", u=2, e=2),
+                func=COPY,
+                scale=-1.0,
+            )
+
+        def quantize_z(b0, b1, engine_copy):
+            n = (b1 - b0) * P
+            back = work.tile([P, 2, n], F32, name="back%d" % b0, tag="work")
+            for b in range(b0, b1):
+                for u in range(2):
+                    words = z_rows[b][:, u].rearrange("v p e -> v (p e)").bitcast(F32)
+                    nc.tensor.transpose(back[:, u, (b - b0) * P : (b - b0 + 1) * P], words, ident[:])
+            z_woven = keep.tile([P, n * PACK], BF16, name="z_woven%d" % b0, tag="woven%d" % b0, align_bytes=64)
+            engine_copy(
+                out=z_woven[:].bitcast(F32).rearrange("p (v u) -> p v u", u=2), in_=back[:].rearrange("p u v -> p v u")
+            )
+            z_codes = keep.tile([P, n], U32, name="z_codes%d" % b0, align_bytes=64)
+            z_plane = keep.tile([P, n], U8, name="z_plane%d" % b0, align_bytes=64)
+            nc.vector.quantize_mx(out=z_codes[:].bitcast(FP8X4), scales=z_plane[:], in_=z_woven[:])
+            return z_codes, z_plane
+
+        def finish(b0, b1, z_codes, z_plane, engine_copy):
+            n = (b1 - b0) * P
+            acc = work.tile([P, N // P, n], F32, name="out_acc%d" % b0, tag="work")
+            for m in range(N // P):
+                nc.tensor.matmul_mx(
+                    out=acc[:, m, :],
+                    lhsT=w2_codes[:, m * P : (m + 1) * P].bitcast(FP8X4),
+                    lhsT_scale=w2_plane[:, m * P : (m + 1) * P],
+                    rhs=z_codes[:].bitcast(FP8X4),
+                    rhs_scale=z_plane[:],
+                    start=True,
+                    stop=True,
+                )
+            result = keep.tile([P, N // P, n], F32, name="result%d" % b0)
+            engine_copy(out=result[:], in_=acc[:])
+            nc.sync.dma_start(out=out.rearrange("(m p) v -> p m v", p=P)[:, :, b0 * P : b1 * P], in_=result[:])
+
+        quantize_w1_first()
+        acc0 = project(0)
+        acc1 = project(1)
+        negate(0, acc0)
+        negate(1, acc1)
+        for d in range(D):
+            gather(0, d, 0, VBLOCKS)
+        gather(1, 0, 0, VBLOCKS)
+        quantize_w1(2, nc.scalar.copy, "chain0")
+        negate(2, project(2))
+        gather(1, 1, 0, VBLOCKS, "chain0")
+        quantize_w1(3, nc.scalar.copy, "chain1")
+        negate(3, project(3))
+        gather(1, 2, 0, VBLOCKS, "chain1")
+        for b in range(VBLOCKS):
+            round_z(b, 0, 2)
+
+        for j in (2, 3):
+            for d in range(D):
+                gather(j, d, 0, 2)
+        for b in (0, 1):
+            round_z(b, 2, 4)
+        z01 = quantize_z(0, 2, nc.scalar.copy)
+        finish(0, 2, z01[0], z01[1], nc.scalar.copy)
+        for j in (2, 3):
+            for d in range(D):
+                gather(j, d, 2, 3)
+        round_z(2, 2, 4)
+        z2 = quantize_z(2, 3, nc.scalar.copy)
+        for d in range(D):
+            gather(2, d, 3, 4)
+        round_z(3, 2, 3)
+        gather(3, 0, 3, 4, "woven0")
+        gather(3, 1, 3, 4, "rows2")
+        gather(3, 2, 3, 4)
+        round_z(3, 3, 4)
+        finish(2, 3, z2[0], z2[1], nc.scalar.copy)
+        z3 = quantize_z(3, 4, nc.vector.tensor_copy)
+        finish(3, 4, z3[0], z3[1], nc.vector.tensor_copy)

@@ -36,12 +36,6 @@ def tile_picked_wlapl_none_l_kernel(
         x_plane = keep.tile([P, PASSES, T], U8, name="x_plane", align_bytes=64)
         w2_plane = keep.tile([P, N], U8, name="w2_plane", align_bytes=64)
         nc.gpsimd.memset(x_plane[:].rearrange("p g c -> p (g c)").bitcast(U32), 0)
-        nc.gpsimd.memset(w2_plane[:].bitcast(U32), 0)
-        ident = keep.tile([P, P], F32, name="ident")
-        make_identity(nc, ident[:])
-        h = [keep.tile([P, T + SPARE], F32, name="h%d" % j) for j in range(BLOCKS)]
-        for j in range(BLOCKS):
-            nc.gpsimd.memset(h[j][:, T:], 0.0)
 
         w1_raw = {}
 
@@ -64,11 +58,14 @@ def tile_picked_wlapl_none_l_kernel(
                 out=x_plane[32 * q : 32 * q + 4].bitcast(I32),
                 in_=x_scales[:, 4 * q : 4 * q + 4, :].rearrange("g r c -> r g c").bitcast(I32),
             )
-        x_codes = []
-        for g in range(PASSES):
-            codes = keep.tile([P, T], U32, name="x_codes%d" % g, align_bytes=64)
-            nc.sync.dma_start(out=codes[:].bitcast(I32), in_=x_words[g].rearrange("p c r -> p (c r)").bitcast(I32))
-            x_codes.append(codes)
+        nc.gpsimd.memset(w2_plane[:].bitcast(U32), 0)
+        h = [keep.tile([P, T + SPARE], F32, name="h%d" % j) for j in range(BLOCKS)]
+        for j in range(BLOCKS):
+            nc.gpsimd.memset(h[j][:, T:], 0.0)
+        ident = keep.tile([P, P], F32, name="ident")
+        make_identity(nc, ident[:])
+        x_codes = keep.tile([P, PASSES, T], U32, name="x_codes", align_bytes=64)
+        nc.sync.dma_start(out=x_codes[:].bitcast(I32), in_=x_words.rearrange("g p c r -> p g (c r)").bitcast(I32))
         lists = [load_list(0, pos1)]
         gate_first = keep.tile([P, T], F32, name="gate_first")
         gate_rest = keep.tile([P, D - 1, T], F32, name="gate_rest")
@@ -89,8 +86,8 @@ def tile_picked_wlapl_none_l_kernel(
 
         def weave(engine_copy, dst, raw):
             engine_copy(
-                out=dst.rearrange("p (c i t) -> p c t i", i=4, t=PACK),
-                in_=raw.rearrange("p t (c i) -> p c t i", i=4),
+                out=dst.rearrange("p (c t) -> p c t", t=PACK),
+                in_=raw.rearrange("p t c -> p c t"),
             )
 
         w1_codes = [keep.tile([P, PASSES, P], U32, name="w1_codes%d" % j, tag="chain%d" % j, align_bytes=64) for j in range(BLOCKS)]
@@ -125,7 +122,7 @@ def tile_picked_wlapl_none_l_kernel(
                     out=acc[:],
                     lhsT=w1_codes[j][:, g, :].bitcast(FP8X4),
                     lhsT_scale=w1_plane[j][:, g, :],
-                    rhs=x_codes[g][:].bitcast(FP8X4),
+                    rhs=x_codes[:, g, :].bitcast(FP8X4),
                     rhs_scale=x_plane[:, g, :],
                     start=(g == 0),
                     stop=(g == PASSES - 1),
@@ -144,15 +141,19 @@ def tile_picked_wlapl_none_l_kernel(
                 out=turned[b][:, j * P : (j + 1) * P], lhsT=term, rhs=ident[:], start=first, stop=last, is_transpose=True
             )
 
-        def gather(j, d, b0, b1, tag=None):
+        def gather(j, d, b0, b1, tag=None, term=None):
             v0, v1 = b0 * P, b1 * P
-            term = keep.tile([P, v1 - v0], F32, name="term%d_%d_%d" % (j, d, b0), tag=tag or "term%d_%d_%d" % (j, d, b0), align_bytes=64)
+            if term is None:
+                name = "term%d_%d_%d" % (j, d, b0)
+                term = keep.tile([P, v1 - v0], F32, name=name, tag=tag or name, align_bytes=64)[:]
             window = h[j][:].indirect(lists[d][:, v0 // 16 : v1 // 16])
-            nc.vector.tensor_tensor(term[:], window, gates[d][:, v0:v1], MULT)
+            nc.vector.tensor_tensor(term, window, gates[d][:, v0:v1], MULT)
             for b in range(b0, b1):
-                if d == 0:
+                if d == 0 and j != 1:
                     add_turned(j, b, minus_h[j][:, b * P : (b + 1) * P], True, False)
-                add_turned(j, b, term[:, (b - b0) * P : (b - b0 + 1) * P], False, d == D - 1)
+                add_turned(j, b, term[:, (b - b0) * P : (b - b0 + 1) * P], False, d == D - 1 and j != 0)
+                if d == 0 and j == 0:
+                    add_turned(1, b, minus_h[1][:, b * P : (b + 1) * P], False, False)
 
         def round_z(b, j0, j1):
             nc.scalar.activation(
@@ -219,13 +220,16 @@ def tile_picked_wlapl_none_l_kernel(
             round_z(b, 2, 4)
         z01 = quantize_z(0, 2, nc.scalar.copy)
         finish(0, 2, z01[0], z01[1], nc.scalar.copy)
-        for j in (2, 3):
-            for d in range(D):
-                gather(j, d, 2, 3)
+        held2 = keep.tile([P, D, P], F32, name="held2", tag="term3_0_0", align_bytes=64)
+        for d in range(D):
+            gather(2, d, 2, 3, term=held2[:, d, :])
+        for d in range(D):
+            gather(3, d, 2, 3)
         round_z(2, 2, 4)
         z2 = quantize_z(2, 3, nc.scalar.copy)
+        held3 = keep.tile([P, D, P], F32, name="held3", tag="term3_1_0", align_bytes=64)
         for d in range(D):
-            gather(2, d, 3, 4)
+            gather(2, d, 3, 4, term=held3[:, d, :])
         round_z(3, 2, 3)
         gather(3, 0, 3, 4, "woven0")
         gather(3, 1, 3, 4, "rows2")

@@ -22,6 +22,8 @@ PASSES = K // (P * PACK)
 BLOCKS = H // P
 VBLOCKS = T // P
 SPARE = 16
+HALF = T // 2
+SHARE = 80
 
 
 def tile_picked_wlapl_none_l_kernel(
@@ -51,28 +53,30 @@ def tile_picked_wlapl_none_l_kernel(
             nc.sync.dma_start(offsets[:], pos)
             return offsets
 
-        for g in range(PASSES):
-            load_w1(0, 2, g)
+        load_w1(0, 2, 0)
         for q in range(4):
             (nc.scalar if q < 2 else nc.sync).dma_start(
                 out=x_plane[32 * q : 32 * q + 4].bitcast(I32),
                 in_=x_scales[:, 4 * q : 4 * q + 4, :].rearrange("g r c -> r g c").bitcast(I32),
             )
+        load_w1(0, 2, 1)
         nc.gpsimd.memset(w2_plane[:].bitcast(U32), 0)
         h = [keep.tile([P, T + SPARE], F32, name="h%d" % j) for j in range(BLOCKS)]
         for j in range(BLOCKS):
             nc.gpsimd.memset(h[j][:, T:], 0.0)
         ident = keep.tile([P, P], F32, name="ident")
         make_identity(nc, ident[:])
-        x_codes = keep.tile([P, PASSES, T], U32, name="x_codes", align_bytes=64)
-        nc.sync.dma_start(out=x_codes[:].bitcast(I32), in_=x_words.rearrange("g p c r -> p g (c r)").bitcast(I32))
-        lists = [load_list(0, pos1)]
+        x_codes = []
+        for a in range(2):
+            codes = keep.tile([P, PASSES, HALF], U32, name="x_codes%d" % a, align_bytes=64)
+            columns = x_words[:, :, a * HALF : (a + 1) * HALF, :]
+            nc.sync.dma_start(out=codes[:].bitcast(I32), in_=columns.rearrange("g p c r -> p g (c r)").bitcast(I32))
+            x_codes.append(codes)
         gate_first = keep.tile([P, T], F32, name="gate_first")
         gate_rest = keep.tile([P, D - 1, T], F32, name="gate_rest")
         gates = [gate_first[:]] + [gate_rest[:, d, :] for d in range(D - 1)]
         nc.sync.dma_start(out=gate_first[:], in_=gate[0])
-        lists.append(load_list(1, pos2))
-        lists.append(load_list(2, pos3))
+        lists = [load_list(d, pos) for d, pos in enumerate((pos1, pos2, pos3))]
         nc.sync.dma_start(out=gate_rest[:], in_=gate[1:].rearrange("d p v -> p d v"))
         for g in range(PASSES):
             load_w1(2, BLOCKS, g)
@@ -90,50 +94,67 @@ def tile_picked_wlapl_none_l_kernel(
                 in_=raw.rearrange("p t c -> p c t"),
             )
 
-        w1_codes = [keep.tile([P, PASSES, P], U32, name="w1_codes%d" % j, tag="chain%d" % j, align_bytes=64) for j in range(BLOCKS)]
-        w1_plane = [keep.tile([P, PASSES, P], U8, name="w1_plane%d" % j, align_bytes=64) for j in range(BLOCKS)]
+        w1_codes = [keep.tile([P, PASSES, P], U32, name="w1_codes%d" % j, tag="chain%d" % j, align_bytes=64)[:] for j in range(2)]
+        w1_plane = [keep.tile([P, PASSES, P], U8, name="w1_plane%d" % j, align_bytes=64)[:] for j in range(2)]
+        late_codes = keep.tile([P, 2, PASSES, P], U32, name="late_codes", align_bytes=64)
+        late_plane = keep.tile([P, 2, PASSES, P], U8, name="late_plane", align_bytes=64)
+        w1_codes.extend(late_codes[:, j] for j in range(2))
+        w1_plane.extend(late_plane[:, j] for j in range(2))
 
         def quantize_w1_first():
             for g in range(PASSES):
                 woven = [keep.tile([P, P * PACK], BF16, name="w1_first%d_%d" % (j, g), align_bytes=64) for j in range(2)]
-                for j in range(2):
-                    weave(nc.vector.tensor_copy, woven[j][:], w1_raw[j, g])
+                weave(nc.vector.tensor_copy, woven[0][:, : SHARE * PACK], w1_raw[0, g][:, :, :SHARE])
+                weave(nc.scalar.copy, woven[0][:, SHARE * PACK :], w1_raw[0, g][:, :, SHARE:])
+                weave(nc.scalar.copy, woven[1][:], w1_raw[1, g])
                 for j in range(2):
                     nc.vector.quantize_mx(
                         out=w1_codes[j][:, g, :].bitcast(FP8X4), scales=w1_plane[j][:, g, :], in_=woven[j][:]
                     )
 
-        def quantize_w1(j, engine_copy, tag):
-            woven = keep.tile([P, PASSES, P * PACK], BF16, name="w1_woven%d" % j, tag=tag, align_bytes=64)
+        def quantize_w1_late():
+            woven = keep.tile([P, 2, PASSES, P * PACK], BF16, name="w1_late", tag="chain1", align_bytes=64)
             for g in range(PASSES):
-                weave(engine_copy, woven[:, g, :], w1_raw[j, g])
+                for j in range(2):
+                    weave(nc.scalar.copy, woven[:, j, g, :], w1_raw[2 + j, g])
             nc.vector.quantize_mx(
-                out=w1_codes[j][:].rearrange("p g c -> p (g c)").bitcast(FP8X4),
-                scales=w1_plane[j][:].rearrange("p g c -> p (g c)"),
-                in_=woven[:].rearrange("p g c -> p (g c)"),
+                out=late_codes[:].rearrange("p j g c -> p (j g c)").bitcast(FP8X4),
+                scales=late_plane[:].rearrange("p j g c -> p (j g c)"),
+                in_=woven[:].rearrange("p j g c -> p (j g c)"),
             )
 
         minus_h = [keep.tile([P, T], F32, name="minus_h%d" % j) for j in range(BLOCKS)]
 
-        def project(j):
-            acc = work.tile([P, T], F32, name="h_acc%d" % j, tag="work")
+        def multiply_w1(j, a, acc):
             for g in range(PASSES):
                 nc.tensor.matmul_mx(
-                    out=acc[:],
+                    out=acc,
                     lhsT=w1_codes[j][:, g, :].bitcast(FP8X4),
                     lhsT_scale=w1_plane[j][:, g, :],
-                    rhs=x_codes[:, g, :].bitcast(FP8X4),
-                    rhs_scale=x_plane[:, g, :],
+                    rhs=x_codes[a][:, g, :].bitcast(FP8X4),
+                    rhs_scale=x_plane[:, g, a * HALF : (a + 1) * HALF],
                     start=(g == 0),
                     stop=(g == PASSES - 1),
                 )
+
+        def project_first():
+            for a in range(2):
+                acc = work.tile([P, HALF], F32, name="h_first%d" % a, tag="work")
+                multiply_w1(0, a, acc[:])
+                nc.scalar.copy(out=h[0][:, a * HALF : (a + 1) * HALF], in_=acc[:])
+            nc.scalar.activation(out=minus_h[0][:], in_=h[0][:, :T], func=COPY, scale=-1.0)
+
+        def project(j):
+            acc = work.tile([P, T], F32, name="h_acc%d" % j, tag="work")
+            for a in range(2):
+                multiply_w1(j, a, acc[:, a * HALF : (a + 1) * HALF])
             nc.scalar.copy(out=h[j][:, :T], in_=acc[:])
             return acc
 
         def negate(j, acc):
             nc.scalar.activation(out=minus_h[j][:], in_=acc[:], func=COPY, scale=-1.0)
 
-        turned = [sums.tile([P, H], F32, name="turned%d" % b) for b in range(VBLOCKS)]
+        turned = [sums.tile([P, H], F32, name="turned%d" % b, tag="turned%d" % b) for b in range(VBLOCKS)]
         z_rows = [keep.tile([P, 2, P, 2], BF16, name="z_rows%d" % b, tag="rows%d" % b, align_bytes=64) for b in range(VBLOCKS)]
 
         def add_turned(j, b, term, first, last):
@@ -179,37 +200,47 @@ def tile_picked_wlapl_none_l_kernel(
             nc.vector.quantize_mx(out=z_codes[:].bitcast(FP8X4), scales=z_plane[:], in_=z_woven[:])
             return z_codes, z_plane
 
-        def finish(b0, b1, z_codes, z_plane, engine_copy):
+        def multiply_w2(m, z_codes, z_plane, acc):
+            nc.tensor.matmul_mx(
+                out=acc,
+                lhsT=w2_codes[:, m * P : (m + 1) * P].bitcast(FP8X4),
+                lhsT_scale=w2_plane[:, m * P : (m + 1) * P],
+                rhs=z_codes[:].bitcast(FP8X4),
+                rhs_scale=z_plane[:],
+                start=True,
+                stop=True,
+            )
+
+        def finish(b0, b1, z_codes, z_plane, tag):
             n = (b1 - b0) * P
             acc = work.tile([P, N // P, n], F32, name="out_acc%d" % b0, tag="work")
             for m in range(N // P):
-                nc.tensor.matmul_mx(
-                    out=acc[:, m, :],
-                    lhsT=w2_codes[:, m * P : (m + 1) * P].bitcast(FP8X4),
-                    lhsT_scale=w2_plane[:, m * P : (m + 1) * P],
-                    rhs=z_codes[:].bitcast(FP8X4),
-                    rhs_scale=z_plane[:],
-                    start=True,
-                    stop=True,
-                )
-            result = keep.tile([P, N // P, n], F32, name="result%d" % b0)
-            engine_copy(out=result[:], in_=acc[:])
+                multiply_w2(m, z_codes, z_plane, acc[:, m, :])
+            result = keep.tile([P, N // P, n], F32, name="result%d" % b0, tag=tag, align_bytes=64)
+            nc.scalar.copy(out=result[:], in_=acc[:])
             nc.sync.dma_start(out=out.rearrange("(m p) v -> p m v", p=P)[:, :, b0 * P : b1 * P], in_=result[:])
 
+        def finish_last(b, z_codes, z_plane):
+            for m, (engine_copy, queue) in enumerate(((nc.vector.tensor_copy, nc.sync), (nc.scalar.copy, nc.scalar))):
+                acc = work.tile([P, P], F32, name="last_acc%d" % m, tag="work")
+                multiply_w2(m, z_codes, z_plane, acc[:])
+                result = keep.tile([P, P], F32, name="last_result%d" % m)
+                engine_copy(out=result[:], in_=acc[:])
+                queue.dma_start(out=out[m * P : (m + 1) * P, b * P : (b + 1) * P], in_=result[:])
+
         quantize_w1_first()
-        acc0 = project(0)
-        acc1 = project(1)
-        negate(0, acc0)
-        negate(1, acc1)
+        project_first()
+        negate(1, project(1))
         for d in range(D):
             gather(0, d, 0, VBLOCKS)
         gather(1, 0, 0, VBLOCKS)
-        quantize_w1(2, nc.scalar.copy, "chain0")
-        negate(2, project(2))
-        gather(1, 1, 0, VBLOCKS, "chain0")
-        quantize_w1(3, nc.scalar.copy, "chain1")
-        negate(3, project(3))
-        gather(1, 2, 0, VBLOCKS, "chain1")
+        quantize_w1_late()
+        late = [project(j) for j in (2, 3)]
+        for j in (2, 3):
+            negate(j, late[j - 2])
+        held = keep.tile([P, D - 1, T], F32, name="held", tag="chain1", align_bytes=64)
+        for d in range(1, D):
+            gather(1, d, 0, VBLOCKS, term=held[:, d - 1, :])
         for b in range(VBLOCKS):
             round_z(b, 0, 2)
 
@@ -219,22 +250,22 @@ def tile_picked_wlapl_none_l_kernel(
         for b in (0, 1):
             round_z(b, 2, 4)
         z01 = quantize_z(0, 2, nc.scalar.copy)
-        finish(0, 2, z01[0], z01[1], nc.scalar.copy)
-        held2 = keep.tile([P, D, P], F32, name="held2", tag="term3_0_0", align_bytes=64)
+        finish(0, 2, z01[0], z01[1], "result0")
+        held_a = keep.tile([P, D, HALF], F32, name="held_a", tag="term3_0_0", align_bytes=64)
         for d in range(D):
-            gather(2, d, 2, 3, term=held2[:, d, :])
-        for d in range(D):
-            gather(3, d, 2, 3)
-        round_z(2, 2, 4)
-        z2 = quantize_z(2, 3, nc.scalar.copy)
-        held3 = keep.tile([P, D, P], F32, name="held3", tag="term3_1_0", align_bytes=64)
-        for d in range(D):
-            gather(2, d, 3, 4, term=held3[:, d, :])
+            gather(2, d, 2, 4, term=held_a[:, d, :])
+        round_z(2, 2, 3)
         round_z(3, 2, 3)
-        gather(3, 0, 3, 4, "woven0")
-        gather(3, 1, 3, 4, "rows2")
-        gather(3, 2, 3, 4)
+        held_b = keep.tile([P, D - 1, P], F32, name="held_b", tag="rows1", align_bytes=64)
+        held_c = keep.tile([P, D + 1, P], F32, name="held_c", tag="woven0", align_bytes=64)
+        for d in range(D - 1):
+            gather(3, d, 2, 3, term=held_b[:, d, :])
+        gather(3, D - 1, 2, 3, term=held_c[:, D, :])
+        round_z(2, 3, 4)
+        z2 = quantize_z(2, 3, nc.vector.tensor_copy)
+        for d in range(D):
+            gather(3, d, 3, 4, term=held_c[:, d, :])
         round_z(3, 3, 4)
-        finish(2, 3, z2[0], z2[1], nc.scalar.copy)
-        z3 = quantize_z(3, 4, nc.vector.tensor_copy)
-        finish(3, 4, z3[0], z3[1], nc.vector.tensor_copy)
+        z3 = quantize_z(3, 4, nc.scalar.copy)
+        finish(2, 3, z2[0], z2[1], "rows3")
+        finish_last(3, *z3)

@@ -18,12 +18,16 @@ MULT = mybir.AluOpType.mult
 
 P = 128
 PACK = 4
+QUADRANT = 32
+STRIPE = 16
 PASSES = K // (P * PACK)
-BLOCKS = H // P
-VBLOCKS = T // P
+CHANNEL_BLOCKS = H // P
+TARGET_BLOCKS = T // P
+EARLY = 2
 SPARE = 16
 HALF = T // 2
-SHARE = 80
+VECTOR_COLUMNS = 80
+WORK_BANKS = 4
 
 
 def tile_picked_wlapl_none_l_kernel(
@@ -33,7 +37,7 @@ def tile_picked_wlapl_none_l_kernel(
     with ExitStack() as ctx:
         keep = ctx.enter_context(tc.tile_pool(name="keep", bufs=1))
         sums = ctx.enter_context(tc.psum_pool(name="sums", bufs=1))
-        work = ctx.enter_context(tc.psum_pool(name="work", bufs=4))
+        work = ctx.enter_context(tc.psum_pool(name="work", bufs=WORK_BANKS))
 
         x_plane = keep.tile([P, PASSES, T], U8, name="x_plane", align_bytes=64)
         w2_plane = keep.tile([P, N], U8, name="w2_plane", align_bytes=64)
@@ -49,20 +53,20 @@ def tile_picked_wlapl_none_l_kernel(
                 w1_raw[j, g] = raw[:, :, (j - j0) * P : (j - j0 + 1) * P]
 
         def load_list(d, pos):
-            offsets = keep.tile([P, T // 16], U16, name="offsets%d" % d)
+            offsets = keep.tile([P, T // STRIPE], U16, name="offsets%d" % d)
             nc.sync.dma_start(offsets[:], pos)
             return offsets
 
-        load_w1(0, 2, 0)
-        for q in range(4):
-            (nc.scalar if q < 2 else nc.sync).dma_start(
-                out=x_plane[32 * q : 32 * q + 4].bitcast(I32),
+        load_w1(0, EARLY, 0)
+        for q, queue in enumerate((nc.scalar, nc.scalar, nc.sync, nc.sync)):
+            queue.dma_start(
+                out=x_plane[QUADRANT * q : QUADRANT * q + 4].bitcast(I32),
                 in_=x_scales[:, 4 * q : 4 * q + 4, :].rearrange("g r c -> r g c").bitcast(I32),
             )
-        load_w1(0, 2, 1)
+        load_w1(0, EARLY, 1)
         nc.gpsimd.memset(w2_plane[:].bitcast(U32), 0)
-        h = [keep.tile([P, T + SPARE], F32, name="h%d" % j) for j in range(BLOCKS)]
-        for j in range(BLOCKS):
+        h = [keep.tile([P, T + SPARE], F32, name="h%d" % j) for j in range(CHANNEL_BLOCKS)]
+        for j in range(CHANNEL_BLOCKS):
             nc.gpsimd.memset(h[j][:, T:], 0.0)
         ident = keep.tile([P, P], F32, name="ident")
         make_identity(nc, ident[:])
@@ -79,51 +83,55 @@ def tile_picked_wlapl_none_l_kernel(
         lists = [load_list(d, pos) for d, pos in enumerate((pos1, pos2, pos3))]
         nc.sync.dma_start(out=gate_rest[:], in_=gate[1:].rearrange("d p v -> p d v"))
         for g in range(PASSES):
-            load_w1(2, BLOCKS, g)
+            load_w1(EARLY, CHANNEL_BLOCKS, g)
         w2_codes = keep.tile([P, N], U32, name="w2_codes", align_bytes=64)
         nc.sync.dma_start(out=w2_codes[:].bitcast(I32), in_=w2_words[0].rearrange("p c r -> p (c r)").bitcast(I32))
-        for q in range(4):
+        for q in range(P // QUADRANT):
             nc.sync.dma_start(
-                out=w2_plane[32 * q : 32 * q + 4].bitcast(I32),
+                out=w2_plane[QUADRANT * q : QUADRANT * q + 4].bitcast(I32),
                 in_=w2_scales[0, 4 * q : 4 * q + 4, :].bitcast(I32),
             )
 
-        def weave(engine_copy, dst, raw):
-            engine_copy(
-                out=dst.rearrange("p (c t) -> p c t", t=PACK),
-                in_=raw.rearrange("p t c -> p c t"),
-            )
+        def interleave(engine_copy, dst, raw):
+            engine_copy(out=dst.rearrange("p (c t) -> p c t", t=PACK), in_=raw.rearrange("p t c -> p c t"))
 
-        w1_codes = [keep.tile([P, PASSES, P], U32, name="w1_codes%d" % j, tag="chain%d" % j, align_bytes=64)[:] for j in range(2)]
-        w1_plane = [keep.tile([P, PASSES, P], U8, name="w1_plane%d" % j, align_bytes=64)[:] for j in range(2)]
-        late_codes = keep.tile([P, 2, PASSES, P], U32, name="late_codes", align_bytes=64)
-        late_plane = keep.tile([P, 2, PASSES, P], U8, name="late_plane", align_bytes=64)
-        w1_codes.extend(late_codes[:, j] for j in range(2))
-        w1_plane.extend(late_plane[:, j] for j in range(2))
+        late = CHANNEL_BLOCKS - EARLY
+        w1_codes = [
+            keep.tile([P, PASSES, P], U32, name="w1_codes%d" % j, tag="w1_codes%d" % j, align_bytes=64)[:]
+            for j in range(EARLY)
+        ]
+        w1_plane = [keep.tile([P, PASSES, P], U8, name="w1_plane%d" % j, align_bytes=64)[:] for j in range(EARLY)]
+        late_codes = keep.tile([P, late, PASSES, P], U32, name="late_codes", align_bytes=64)
+        late_plane = keep.tile([P, late, PASSES, P], U8, name="late_plane", align_bytes=64)
+        w1_codes.extend(late_codes[:, n] for n in range(late))
+        w1_plane.extend(late_plane[:, n] for n in range(late))
 
-        def quantize_w1_first():
+        def quantize_w1_early():
+            cut = VECTOR_COLUMNS
             for g in range(PASSES):
-                woven = [keep.tile([P, P * PACK], BF16, name="w1_first%d_%d" % (j, g), align_bytes=64) for j in range(2)]
-                weave(nc.vector.tensor_copy, woven[0][:, : SHARE * PACK], w1_raw[0, g][:, :, :SHARE])
-                weave(nc.scalar.copy, woven[0][:, SHARE * PACK :], w1_raw[0, g][:, :, SHARE:])
-                weave(nc.scalar.copy, woven[1][:], w1_raw[1, g])
-                for j in range(2):
+                rounded = [
+                    keep.tile([P, P * PACK], BF16, name="w1_early%d_%d" % (j, g), align_bytes=64) for j in range(EARLY)
+                ]
+                interleave(nc.vector.tensor_copy, rounded[0][:, : cut * PACK], w1_raw[0, g][:, :, :cut])
+                interleave(nc.scalar.copy, rounded[0][:, cut * PACK :], w1_raw[0, g][:, :, cut:])
+                interleave(nc.scalar.copy, rounded[1][:], w1_raw[1, g])
+                for j in range(EARLY):
                     nc.vector.quantize_mx(
-                        out=w1_codes[j][:, g, :].bitcast(FP8X4), scales=w1_plane[j][:, g, :], in_=woven[j][:]
+                        out=w1_codes[j][:, g, :].bitcast(FP8X4), scales=w1_plane[j][:, g, :], in_=rounded[j][:]
                     )
 
         def quantize_w1_late():
-            woven = keep.tile([P, 2, PASSES, P * PACK], BF16, name="w1_late", tag="chain1", align_bytes=64)
+            rounded = keep.tile([P, late, PASSES, P * PACK], BF16, name="w1_late", tag="w1_codes1", align_bytes=64)
             for g in range(PASSES):
-                for j in range(2):
-                    weave(nc.scalar.copy, woven[:, j, g, :], w1_raw[2 + j, g])
+                for n in range(late):
+                    interleave(nc.scalar.copy, rounded[:, n, g, :], w1_raw[EARLY + n, g])
             nc.vector.quantize_mx(
-                out=late_codes[:].rearrange("p j g c -> p (j g c)").bitcast(FP8X4),
-                scales=late_plane[:].rearrange("p j g c -> p (j g c)"),
-                in_=woven[:].rearrange("p j g c -> p (j g c)"),
+                out=late_codes[:].rearrange("p n g c -> p (n g c)").bitcast(FP8X4),
+                scales=late_plane[:].rearrange("p n g c -> p (n g c)"),
+                in_=rounded[:].rearrange("p n g c -> p (n g c)"),
             )
 
-        minus_h = [keep.tile([P, T], F32, name="minus_h%d" % j) for j in range(BLOCKS)]
+        minus_h = [keep.tile([P, T], F32, name="minus_h%d" % j) for j in range(CHANNEL_BLOCKS)]
 
         def multiply_w1(j, a, acc):
             for g in range(PASSES):
@@ -142,44 +150,50 @@ def tile_picked_wlapl_none_l_kernel(
                 acc = work.tile([P, HALF], F32, name="h_first%d" % a, tag="work")
                 multiply_w1(0, a, acc[:])
                 nc.scalar.copy(out=h[0][:, a * HALF : (a + 1) * HALF], in_=acc[:])
-            nc.scalar.activation(out=minus_h[0][:], in_=h[0][:, :T], func=COPY, scale=-1.0)
 
         def project(j):
             acc = work.tile([P, T], F32, name="h_acc%d" % j, tag="work")
             for a in range(2):
                 multiply_w1(j, a, acc[:, a * HALF : (a + 1) * HALF])
             nc.scalar.copy(out=h[j][:, :T], in_=acc[:])
-            return acc
+            return acc[:]
 
-        def negate(j, acc):
-            nc.scalar.activation(out=minus_h[j][:], in_=acc[:], func=COPY, scale=-1.0)
+        def negate(j, h_rows):
+            nc.scalar.activation(out=minus_h[j][:], in_=h_rows, func=COPY, scale=-1.0)
 
-        turned = [sums.tile([P, H], F32, name="turned%d" % b, tag="turned%d" % b) for b in range(VBLOCKS)]
-        z_rows = [keep.tile([P, 2, P, 2], BF16, name="z_rows%d" % b, tag="rows%d" % b, align_bytes=64) for b in range(VBLOCKS)]
+        minus_z = [sums.tile([P, H], F32, name="minus_z%d" % b) for b in range(TARGET_BLOCKS)]
+        z_pairs = [
+            keep.tile([P, 2, P, 2], BF16, name="z_pairs%d" % b, tag="z_pairs%d" % b, align_bytes=64)
+            for b in range(TARGET_BLOCKS)
+        ]
 
-        def add_turned(j, b, term, first, last):
+        def add_transposed(j, b, term, first, last):
             nc.tensor.matmul(
-                out=turned[b][:, j * P : (j + 1) * P], lhsT=term, rhs=ident[:], start=first, stop=last, is_transpose=True
+                out=minus_z[b][:, j * P : (j + 1) * P], lhsT=term, rhs=ident[:], start=first, stop=last, is_transpose=True
             )
 
-        def gather(j, d, b0, b1, tag=None, term=None):
+        def term_tile(name, shape, tag):
+            return keep.tile([P] + shape, F32, name=name, tag=tag, align_bytes=64)
+
+        def gather(j, d, b0, b1, term):
             v0, v1 = b0 * P, b1 * P
-            if term is None:
-                name = "term%d_%d_%d" % (j, d, b0)
-                term = keep.tile([P, v1 - v0], F32, name=name, tag=tag or name, align_bytes=64)[:]
-            window = h[j][:].indirect(lists[d][:, v0 // 16 : v1 // 16])
-            nc.vector.tensor_tensor(term, window, gates[d][:, v0:v1], MULT)
+            neighbours = h[j][:].indirect(lists[d][:, v0 // STRIPE : v1 // STRIPE])
+            nc.vector.tensor_tensor(term, neighbours, gates[d][:, v0:v1], MULT)
+            opens_group, closes_group = j != 1, j != 0
             for b in range(b0, b1):
-                if d == 0 and j != 1:
-                    add_turned(j, b, minus_h[j][:, b * P : (b + 1) * P], True, False)
-                add_turned(j, b, term[:, (b - b0) * P : (b - b0 + 1) * P], False, d == D - 1 and j != 0)
-                if d == 0 and j == 0:
-                    add_turned(1, b, minus_h[1][:, b * P : (b + 1) * P], False, False)
+                if d == 0:
+                    add_transposed(j, b, minus_h[j][:, b * P : (b + 1) * P], opens_group, False)
+                add_transposed(j, b, term[:, (b - b0) * P : (b - b0 + 1) * P], False, d == D - 1 and closes_group)
+
+        def gather_own_tile(j, d, b0, b1):
+            name = "term%d_%d_%d" % (j, d, b0)
+            gather(j, d, b0, b1, term_tile(name, [(b1 - b0) * P], name)[:])
 
         def round_z(b, j0, j1):
+            per_block = P // PACK
             nc.scalar.activation(
-                out=z_rows[b][:, :, 32 * j0 : 32 * j1, :],
-                in_=turned[b][:, j0 * P : j1 * P].rearrange("v (p u e) -> v u p e", u=2, e=2),
+                out=z_pairs[b][:, :, per_block * j0 : per_block * j1, :],
+                in_=minus_z[b][:, j0 * P : j1 * P].rearrange("v (p u e) -> v u p e", u=2, e=2),
                 func=COPY,
                 scale=-1.0,
             )
@@ -189,83 +203,87 @@ def tile_picked_wlapl_none_l_kernel(
             back = work.tile([P, 2, n], F32, name="back%d" % b0, tag="work")
             for b in range(b0, b1):
                 for u in range(2):
-                    words = z_rows[b][:, u].rearrange("v p e -> v (p e)").bitcast(F32)
+                    words = z_pairs[b][:, u].rearrange("v p e -> v (p e)").bitcast(F32)
                     nc.tensor.transpose(back[:, u, (b - b0) * P : (b - b0 + 1) * P], words, ident[:])
-            z_woven = keep.tile([P, n * PACK], BF16, name="z_woven%d" % b0, tag="woven%d" % b0, align_bytes=64)
+            z_quads = keep.tile([P, n * PACK], BF16, name="z_quads%d" % b0, tag="z_quads%d" % b0, align_bytes=64)
             engine_copy(
-                out=z_woven[:].bitcast(F32).rearrange("p (v u) -> p v u", u=2), in_=back[:].rearrange("p u v -> p v u")
+                out=z_quads[:].bitcast(F32).rearrange("p (v u) -> p v u", u=2), in_=back[:].rearrange("p u v -> p v u")
             )
             z_codes = keep.tile([P, n], U32, name="z_codes%d" % b0, align_bytes=64)
             z_plane = keep.tile([P, n], U8, name="z_plane%d" % b0, align_bytes=64)
-            nc.vector.quantize_mx(out=z_codes[:].bitcast(FP8X4), scales=z_plane[:], in_=z_woven[:])
+            nc.vector.quantize_mx(out=z_codes[:].bitcast(FP8X4), scales=z_plane[:], in_=z_quads[:])
             return z_codes, z_plane
 
-        def multiply_w2(m, z_codes, z_plane, acc):
+        def multiply_w2(r, z_mx, acc):
+            z_codes, z_plane = z_mx
             nc.tensor.matmul_mx(
                 out=acc,
-                lhsT=w2_codes[:, m * P : (m + 1) * P].bitcast(FP8X4),
-                lhsT_scale=w2_plane[:, m * P : (m + 1) * P],
+                lhsT=w2_codes[:, r * P : (r + 1) * P].bitcast(FP8X4),
+                lhsT_scale=w2_plane[:, r * P : (r + 1) * P],
                 rhs=z_codes[:].bitcast(FP8X4),
                 rhs_scale=z_plane[:],
                 start=True,
                 stop=True,
             )
 
-        def finish(b0, b1, z_codes, z_plane, tag):
+        def finish(b0, b1, z_mx, tag):
             n = (b1 - b0) * P
             acc = work.tile([P, N // P, n], F32, name="out_acc%d" % b0, tag="work")
-            for m in range(N // P):
-                multiply_w2(m, z_codes, z_plane, acc[:, m, :])
+            for r in range(N // P):
+                multiply_w2(r, z_mx, acc[:, r, :])
             result = keep.tile([P, N // P, n], F32, name="result%d" % b0, tag=tag, align_bytes=64)
             nc.scalar.copy(out=result[:], in_=acc[:])
-            nc.sync.dma_start(out=out.rearrange("(m p) v -> p m v", p=P)[:, :, b0 * P : b1 * P], in_=result[:])
+            nc.sync.dma_start(out=out.rearrange("(r p) v -> p r v", p=P)[:, :, b0 * P : b1 * P], in_=result[:])
 
-        def finish_last(b, z_codes, z_plane):
-            for m, (engine_copy, queue) in enumerate(((nc.vector.tensor_copy, nc.sync), (nc.scalar.copy, nc.scalar))):
-                acc = work.tile([P, P], F32, name="last_acc%d" % m, tag="work")
-                multiply_w2(m, z_codes, z_plane, acc[:])
-                result = keep.tile([P, P], F32, name="last_result%d" % m)
+        def finish_last(b, z_mx):
+            for r, (engine_copy, queue) in enumerate(((nc.vector.tensor_copy, nc.sync), (nc.scalar.copy, nc.scalar))):
+                acc = work.tile([P, P], F32, name="last_acc%d" % r, tag="work")
+                multiply_w2(r, z_mx, acc[:])
+                result = keep.tile([P, P], F32, name="last_result%d" % r)
                 engine_copy(out=result[:], in_=acc[:])
-                queue.dma_start(out=out[m * P : (m + 1) * P, b * P : (b + 1) * P], in_=result[:])
+                queue.dma_start(out=out[r * P : (r + 1) * P, b * P : (b + 1) * P], in_=result[:])
 
-        quantize_w1_first()
+        quantize_w1_early()
         project_first()
-        negate(1, project(1))
-        for d in range(D):
-            gather(0, d, 0, VBLOCKS)
-        gather(1, 0, 0, VBLOCKS)
-        quantize_w1_late()
-        late = [project(j) for j in (2, 3)]
-        for j in (2, 3):
-            negate(j, late[j - 2])
-        held = keep.tile([P, D - 1, T], F32, name="held", tag="chain1", align_bytes=64)
+        h1_acc = project(1)
+        negate(0, h[0][:, :T])
+        negate(1, h1_acc)
+        for j in range(EARLY):
+            gather_own_tile(j, 0, 0, TARGET_BLOCKS)
         for d in range(1, D):
-            gather(1, d, 0, VBLOCKS, term=held[:, d - 1, :])
-        for b in range(VBLOCKS):
-            round_z(b, 0, 2)
+            gather_own_tile(0, d, 0, TARGET_BLOCKS)
+        quantize_w1_late()
+        late_accs = [project(j) for j in range(EARLY, CHANNEL_BLOCKS)]
+        for n in range(late):
+            negate(EARLY + n, late_accs[n])
+        after_late = term_tile("after_late", [D - 1, T], "w1_codes1")
+        for d in range(1, D):
+            gather(1, d, 0, TARGET_BLOCKS, after_late[:, d - 1, :])
+        for b in range(TARGET_BLOCKS):
+            round_z(b, 0, EARLY)
 
-        for j in (2, 3):
+        for j in range(EARLY, CHANNEL_BLOCKS):
             for d in range(D):
-                gather(j, d, 0, 2)
-        for b in (0, 1):
-            round_z(b, 2, 4)
-        z01 = quantize_z(0, 2, nc.scalar.copy)
-        finish(0, 2, z01[0], z01[1], "result0")
-        held_a = keep.tile([P, D, HALF], F32, name="held_a", tag="term3_0_0", align_bytes=64)
+                gather_own_tile(j, d, 0, 2)
+        for b in range(2):
+            round_z(b, EARLY, CHANNEL_BLOCKS)
+        finish(0, 2, quantize_z(0, 2, nc.scalar.copy), "result0")
+
+        after_third = term_tile("after_third", [D, 2 * P], "term3_0_0")
         for d in range(D):
-            gather(2, d, 2, 4, term=held_a[:, d, :])
-        round_z(2, 2, 3)
-        round_z(3, 2, 3)
-        held_b = keep.tile([P, D - 1, P], F32, name="held_b", tag="rows1", align_bytes=64)
-        held_c = keep.tile([P, D + 1, P], F32, name="held_c", tag="woven0", align_bytes=64)
+            gather(2, d, 2, 4, after_third[:, d, :])
+        for b in (2, 3):
+            round_z(b, 2, 3)
+        after_back = term_tile("after_back", [D - 1, P], "z_pairs1")
+        after_quantize = term_tile("after_quantize", [D + 1, P], "z_quads0")
         for d in range(D - 1):
-            gather(3, d, 2, 3, term=held_b[:, d, :])
-        gather(3, D - 1, 2, 3, term=held_c[:, D, :])
+            gather(3, d, 2, 3, after_back[:, d, :])
+        gather(3, D - 1, 2, 3, after_quantize[:, D, :])
         round_z(2, 3, 4)
-        z2 = quantize_z(2, 3, nc.vector.tensor_copy)
+        z_mx2 = quantize_z(2, 3, nc.vector.tensor_copy)
         for d in range(D):
-            gather(3, d, 3, 4, term=held_c[:, d, :])
+            gather(3, d, 3, 4, after_quantize[:, d, :])
         round_z(3, 3, 4)
-        z3 = quantize_z(3, 4, nc.scalar.copy)
-        finish(2, 3, z2[0], z2[1], "rows3")
-        finish_last(3, *z3)
+        z_mx3 = quantize_z(3, 4, nc.scalar.copy)
+        finish(2, 3, z_mx2, "z_pairs3")
+        finish_last(3, z_mx3)

from contextlib import ExitStack

import concourse.mybir as mybir
from concourse.masks import make_identity

K, T, D, H, N = 1024, 512, 3, 512, 256
FLOPS = 2 * K * H * T + 2 * H * N * T

F32 = mybir.dt.float32
BF16 = mybir.dt.bfloat16
I32 = mybir.dt.int32
U32 = mybir.dt.uint32
U16 = mybir.dt.uint16
U8 = mybir.dt.uint8
FP8X4 = mybir.dt.float8_e4m3fn_x4
COPY = mybir.ActivationFunctionType.Copy
MULT = mybir.AluOpType.mult

P = 128
PACK = 4
QUADRANT = 32
STRIPE = 16
PASSES = K // (P * PACK)
CHANNEL_BLOCKS = H // P
TARGET_BLOCKS = T // P
EARLY = 2
SPARE = 16
HALF = T // 2
VECTOR_COLUMNS = 80
WORK_BANKS = 4


def tile_picked_wlapl_none_l_kernel(
    tc, x_words, x_scales, w1, w2_words, w2_scales, gate, pos1, pos2, pos3, out
):
    nc = tc.nc
    with ExitStack() as ctx:
        keep = ctx.enter_context(tc.tile_pool(name="keep", bufs=1))
        sums = ctx.enter_context(tc.psum_pool(name="sums", bufs=1))
        work = ctx.enter_context(tc.psum_pool(name="work", bufs=WORK_BANKS))

        x_plane = keep.tile([P, PASSES, T], U8, name="x_plane", align_bytes=64)
        w2_plane = keep.tile([P, N], U8, name="w2_plane", align_bytes=64)
        nc.gpsimd.memset(x_plane[:].rearrange("p g c -> p (g c)").bitcast(U32), 0)

        w1_raw = {}

        def load_w1(j0, j1, g):
            raw = keep.tile([P, PACK, (j1 - j0) * P], F32, name="w1_raw%d_%d" % (j0, g))
            rows = w1[g * P * PACK : (g + 1) * P * PACK, j0 * P : j1 * P]
            nc.sync.dma_start(out=raw[:], in_=rows.rearrange("(p t) c -> p t c", t=PACK))
            for j in range(j0, j1):
                w1_raw[j, g] = raw[:, :, (j - j0) * P : (j - j0 + 1) * P]

        def load_list(d, pos):
            offsets = keep.tile([P, T // STRIPE], U16, name="offsets%d" % d)
            nc.sync.dma_start(offsets[:], pos)
            return offsets

        load_w1(0, EARLY, 0)
        for q, queue in enumerate((nc.scalar, nc.scalar, nc.sync, nc.sync)):
            queue.dma_start(
                out=x_plane[QUADRANT * q : QUADRANT * q + 4].bitcast(I32),
                in_=x_scales[:, 4 * q : 4 * q + 4, :].rearrange("g r c -> r g c").bitcast(I32),
            )
        load_w1(0, EARLY, 1)
        nc.gpsimd.memset(w2_plane[:].bitcast(U32), 0)
        h = [keep.tile([P, T + SPARE], F32, name="h%d" % j) for j in range(CHANNEL_BLOCKS)]
        for j in range(CHANNEL_BLOCKS):
            nc.gpsimd.memset(h[j][:, T:], 0.0)
        ident = keep.tile([P, P], F32, name="ident")
        make_identity(nc, ident[:])
        x_codes = []
        for a in range(2):
            codes = keep.tile([P, PASSES, HALF], U32, name="x_codes%d" % a, align_bytes=64)
            columns = x_words[:, :, a * HALF : (a + 1) * HALF, :]
            nc.sync.dma_start(out=codes[:].bitcast(I32), in_=columns.rearrange("g p c r -> p g (c r)").bitcast(I32))
            x_codes.append(codes)
        gate_first = keep.tile([P, T], F32, name="gate_first")
        gate_rest = keep.tile([P, D - 1, T], F32, name="gate_rest")
        gates = [gate_first[:]] + [gate_rest[:, d, :] for d in range(D - 1)]
        nc.sync.dma_start(out=gate_first[:], in_=gate[0])
        lists = [load_list(d, pos) for d, pos in enumerate((pos1, pos2, pos3))]
        nc.sync.dma_start(out=gate_rest[:], in_=gate[1:].rearrange("d p v -> p d v"))
        for g in range(PASSES):
            load_w1(EARLY, CHANNEL_BLOCKS, g)
        w2_codes = keep.tile([P, N], U32, name="w2_codes", align_bytes=64)
        nc.sync.dma_start(out=w2_codes[:].bitcast(I32), in_=w2_words[0].rearrange("p c r -> p (c r)").bitcast(I32))
        for q in range(P // QUADRANT):
            nc.sync.dma_start(
                out=w2_plane[QUADRANT * q : QUADRANT * q + 4].bitcast(I32),
                in_=w2_scales[0, 4 * q : 4 * q + 4, :].bitcast(I32),
            )

        def interleave(engine_copy, dst, raw):
            engine_copy(out=dst.rearrange("p (c t) -> p c t", t=PACK), in_=raw.rearrange("p t c -> p c t"))

        late = CHANNEL_BLOCKS - EARLY
        w1_codes = [
            keep.tile([P, PASSES, P], U32, name="w1_codes%d" % j, tag="w1_codes%d" % j, align_bytes=64)[:]
            for j in range(EARLY)
        ]
        w1_plane = [keep.tile([P, PASSES, P], U8, name="w1_plane%d" % j, align_bytes=64)[:] for j in range(EARLY)]
        late_codes = keep.tile([P, late, PASSES, P], U32, name="late_codes", align_bytes=64)
        late_plane = keep.tile([P, late, PASSES, P], U8, name="late_plane", align_bytes=64)
        w1_codes.extend(late_codes[:, n] for n in range(late))
        w1_plane.extend(late_plane[:, n] for n in range(late))

        def quantize_w1_early():
            cut = VECTOR_COLUMNS
            for g in range(PASSES):
                rounded = [
                    keep.tile([P, P * PACK], BF16, name="w1_early%d_%d" % (j, g), align_bytes=64) for j in range(EARLY)
                ]
                interleave(nc.vector.tensor_copy, rounded[0][:, : cut * PACK], w1_raw[0, g][:, :, :cut])
                interleave(nc.scalar.copy, rounded[0][:, cut * PACK :], w1_raw[0, g][:, :, cut:])
                interleave(nc.scalar.copy, rounded[1][:], w1_raw[1, g])
                for j in range(EARLY):
                    nc.vector.quantize_mx(
                        out=w1_codes[j][:, g, :].bitcast(FP8X4), scales=w1_plane[j][:, g, :], in_=rounded[j][:]
                    )

        def quantize_w1_late():
            rounded = keep.tile([P, late, PASSES, P * PACK], BF16, name="w1_late", tag="w1_codes1", align_bytes=64)
            for g in range(PASSES):
                for n in range(late):
                    interleave(nc.scalar.copy, rounded[:, n, g, :], w1_raw[EARLY + n, g])
            nc.vector.quantize_mx(
                out=late_codes[:].rearrange("p n g c -> p (n g c)").bitcast(FP8X4),
                scales=late_plane[:].rearrange("p n g c -> p (n g c)"),
                in_=rounded[:].rearrange("p n g c -> p (n g c)"),
            )

        minus_h = [keep.tile([P, T], F32, name="minus_h%d" % j) for j in range(CHANNEL_BLOCKS)]

        def multiply_w1(j, a, acc):
            for g in range(PASSES):
                nc.tensor.matmul_mx(
                    out=acc,
                    lhsT=w1_codes[j][:, g, :].bitcast(FP8X4),
                    lhsT_scale=w1_plane[j][:, g, :],
                    rhs=x_codes[a][:, g, :].bitcast(FP8X4),
                    rhs_scale=x_plane[:, g, a * HALF : (a + 1) * HALF],
                    start=(g == 0),
                    stop=(g == PASSES - 1),
                )

        def project_first():
            for a in range(2):
                acc = work.tile([P, HALF], F32, name="h_first%d" % a, tag="work")
                multiply_w1(0, a, acc[:])
                nc.scalar.copy(out=h[0][:, a * HALF : (a + 1) * HALF], in_=acc[:])

        def project(j):
            acc = work.tile([P, T], F32, name="h_acc%d" % j, tag="work")
            for a in range(2):
                multiply_w1(j, a, acc[:, a * HALF : (a + 1) * HALF])
            nc.scalar.copy(out=h[j][:, :T], in_=acc[:])
            return acc[:]

        def negate(j, h_rows):
            nc.scalar.activation(out=minus_h[j][:], in_=h_rows, func=COPY, scale=-1.0)

        minus_z = [sums.tile([P, H], F32, name="minus_z%d" % b) for b in range(TARGET_BLOCKS)]
        z_pairs = [
            keep.tile([P, 2, P, 2], BF16, name="z_pairs%d" % b, tag="z_pairs%d" % b, align_bytes=64)
            for b in range(TARGET_BLOCKS)
        ]

        def add_transposed(j, b, term, first, last):
            nc.tensor.matmul(
                out=minus_z[b][:, j * P : (j + 1) * P], lhsT=term, rhs=ident[:], start=first, stop=last, is_transpose=True
            )

        def term_tile(name, shape, tag):
            return keep.tile([P] + shape, F32, name=name, tag=tag, align_bytes=64)

        def gather(j, d, b0, b1, term):
            v0, v1 = b0 * P, b1 * P
            neighbours = h[j][:].indirect(lists[d][:, v0 // STRIPE : v1 // STRIPE])
            nc.vector.tensor_tensor(term, neighbours, gates[d][:, v0:v1], MULT)
            opens_group, closes_group = j != 1, j != 0
            for b in range(b0, b1):
                if d == 0:
                    add_transposed(j, b, minus_h[j][:, b * P : (b + 1) * P], opens_group, False)
                add_transposed(j, b, term[:, (b - b0) * P : (b - b0 + 1) * P], False, d == D - 1 and closes_group)

        def gather_own_tile(j, d, b0, b1):
            name = "term%d_%d_%d" % (j, d, b0)
            gather(j, d, b0, b1, term_tile(name, [(b1 - b0) * P], name)[:])

        def round_z(b, j0, j1):
            per_block = P // PACK
            nc.scalar.activation(
                out=z_pairs[b][:, :, per_block * j0 : per_block * j1, :],
                in_=minus_z[b][:, j0 * P : j1 * P].rearrange("v (p u e) -> v u p e", u=2, e=2),
                func=COPY,
                scale=-1.0,
            )

        def quantize_z(b0, b1, engine_copy):
            n = (b1 - b0) * P
            back = work.tile([P, 2, n], F32, name="back%d" % b0, tag="work")
            for b in range(b0, b1):
                for u in range(2):
                    words = z_pairs[b][:, u].rearrange("v p e -> v (p e)").bitcast(F32)
                    nc.tensor.transpose(back[:, u, (b - b0) * P : (b - b0 + 1) * P], words, ident[:])
            z_quads = keep.tile([P, n * PACK], BF16, name="z_quads%d" % b0, tag="z_quads%d" % b0, align_bytes=64)
            engine_copy(
                out=z_quads[:].bitcast(F32).rearrange("p (v u) -> p v u", u=2), in_=back[:].rearrange("p u v -> p v u")
            )
            z_codes = keep.tile([P, n], U32, name="z_codes%d" % b0, align_bytes=64)
            z_plane = keep.tile([P, n], U8, name="z_plane%d" % b0, align_bytes=64)
            nc.vector.quantize_mx(out=z_codes[:].bitcast(FP8X4), scales=z_plane[:], in_=z_quads[:])
            return z_codes, z_plane

        def multiply_w2(r, z_mx, acc):
            z_codes, z_plane = z_mx
            nc.tensor.matmul_mx(
                out=acc,
                lhsT=w2_codes[:, r * P : (r + 1) * P].bitcast(FP8X4),
                lhsT_scale=w2_plane[:, r * P : (r + 1) * P],
                rhs=z_codes[:].bitcast(FP8X4),
                rhs_scale=z_plane[:],
                start=True,
                stop=True,
            )

        def finish(b0, b1, z_mx, tag):
            n = (b1 - b0) * P
            acc = work.tile([P, N // P, n], F32, name="out_acc%d" % b0, tag="work")
            for r in range(N // P):
                multiply_w2(r, z_mx, acc[:, r, :])
            result = keep.tile([P, N // P, n], F32, name="result%d" % b0, tag=tag, align_bytes=64)
            nc.scalar.copy(out=result[:], in_=acc[:])
            nc.sync.dma_start(out=out.rearrange("(r p) v -> p r v", p=P)[:, :, b0 * P : b1 * P], in_=result[:])

        def finish_last(b, z_mx):
            for r, (engine_copy, queue) in enumerate(((nc.vector.tensor_copy, nc.sync), (nc.scalar.copy, nc.scalar))):
                acc = work.tile([P, P], F32, name="last_acc%d" % r, tag="work")
                multiply_w2(r, z_mx, acc[:])
                result = keep.tile([P, P], F32, name="last_result%d" % r)
                engine_copy(out=result[:], in_=acc[:])
                queue.dma_start(out=out[r * P : (r + 1) * P, b * P : (b + 1) * P], in_=result[:])

        quantize_w1_early()
        project_first()
        h1_acc = project(1)
        negate(0, h[0][:, :T])
        negate(1, h1_acc)
        for j in range(EARLY):
            gather_own_tile(j, 0, 0, TARGET_BLOCKS)
        for d in range(1, D):
            gather_own_tile(0, d, 0, TARGET_BLOCKS)
        quantize_w1_late()
        late_accs = [project(j) for j in range(EARLY, CHANNEL_BLOCKS)]
        for n in range(late):
            negate(EARLY + n, late_accs[n])
        after_late = term_tile("after_late", [D - 1, T], "w1_codes1")
        for d in range(1, D):
            gather(1, d, 0, TARGET_BLOCKS, after_late[:, d - 1, :])
        for b in range(TARGET_BLOCKS):
            round_z(b, 0, EARLY)

        for j in range(EARLY, CHANNEL_BLOCKS):
            for d in range(D):
                gather_own_tile(j, d, 0, 2)
        for b in range(2):
            round_z(b, EARLY, CHANNEL_BLOCKS)
        finish(0, 2, quantize_z(0, 2, nc.scalar.copy), "result0")

        after_third = term_tile("after_third", [D, 2 * P], "term3_0_0")
        for d in range(D):
            gather(2, d, 2, 4, after_third[:, d, :])
        for b in (2, 3):
            round_z(b, 2, 3)
        after_back = term_tile("after_back", [D - 1, P], "z_pairs1")
        after_quantize = term_tile("after_quantize", [D + 1, P], "z_quads0")
        for d in range(D - 1):
            gather(3, d, 2, 3, after_back[:, d, :])
        gather(3, D - 1, 2, 3, after_quantize[:, D, :])
        round_z(2, 3, 4)
        z_mx2 = quantize_z(2, 3, nc.vector.tensor_copy)
        for d in range(D):
            gather(3, d, 3, 4, after_quantize[:, d, :])
        round_z(3, 3, 4)
        z_mx3 = quantize_z(3, 4, nc.scalar.copy)
        finish(2, 3, z_mx2, "z_pairs3")
        finish_last(3, z_mx3)
